import numpy as np
import ml_dtypes


def mxq(x, axis, fmt="e4m3"):
    dtype, down = {"e4m3": (ml_dtypes.float8_e4m3fn, 7), "e5m2": (ml_dtypes.float8_e5m2, 14)}[fmt]
    v = np.moveaxis(np.asarray(x, np.float32).astype(ml_dtypes.bfloat16).astype(np.float64), axis, -1)
    blocks = v.reshape(v.shape[:-1] + (-1, 32))
    amax = np.abs(blocks).max(-1, keepdims=True)
    byte = np.maximum(np.where(amax > 0, np.frexp(amax)[1] - 1 + 127, 0) - down, 1)
    scale = np.exp2(byte - 127.0)
    codes = (blocks / scale).astype(np.float32).astype(dtype).astype(np.float64)
    return np.moveaxis((codes * scale).reshape(v.shape), -1, axis)


WIDE = False


def mx_kscale(k):
    if not WIDE:
        return np.ones(k)
    levels = np.array([10, -10, 5, -5, 0])
    if k % 512:
        return np.exp2(np.random.permutation(np.resize(levels, k // 32))).repeat(32)
    a = np.empty((k // 512, 16))
    for p in range(k // 512):
        a[p, :8] = np.random.permutation(np.resize(levels, 8))
        for g in range(8):
            far = levels[np.abs(levels - a[p, g]) >= 10]
            a[p, g + 8] = far[np.random.randint(len(far))]
    return np.exp2(a.ravel()).repeat(32)


def f64(x):
    return np.asarray(x).astype(np.float64)


def striped8(idx):
    return np.asarray(idx).reshape(8, -1, 16).transpose(0, 2, 1).reshape(128, -1).astype(np.uint16)


def unstriped8(offs):
    return offs.reshape(8, 16, -1).transpose(0, 2, 1).reshape(8, -1).astype(np.int64)


def pick8(x, idx, run):
    r = np.arange(len(x))
    return x[r[:, None], idx[r % (8 * run) // run]]


E2M1 = np.array([0.0, 0.5, 1.0, 1.5, 2.0, 3.0, 4.0, 6.0, -0.0, -0.5, -1.0, -1.5, -2.0, -3.0, -4.0, -6.0])


def pack_weight(w, fmt):
    k, n = w.shape
    w = f64(np.asarray(w, np.float32).astype(ml_dtypes.bfloat16)).reshape(k // 32, 32, n)
    amax = np.abs(w).max(1)
    if fmt == "e4m3":
        byte = np.frexp(amax)[1] - 1 + 127 - 7
    else:
        mant, ex = np.frexp(amax / 6.0)
        byte = np.where(mant > 0.5, ex, ex - 1) + 127
    byte = np.clip(np.where(amax > 0, byte, 1), 1, 254)
    scaled = (w * np.exp2(127.0 - byte)[:, None, :]).reshape(k, n).astype(np.float32)
    by_word = np.ascontiguousarray(scaled.reshape(k // 512, 128, 4, n).transpose(0, 1, 3, 2))
    if fmt == "e4m3":
        words = by_word.astype(ml_dtypes.float8_e4m3fn).view(np.uint8)
    else:
        c = by_word.astype(ml_dtypes.float4_e2m1fn).view(np.uint8) & 0xF
        words = (c[..., 0::2] | (c[..., 1::2] << 4)).reshape(k // 512, 128, 2 * n)
    return np.ascontiguousarray(words), np.ascontiguousarray(byte.astype(np.uint8).reshape(k // 512, 16, n))


def unpack_weight(words, scales, fmt):
    g, _, n = scales.shape
    words = np.ascontiguousarray(words).reshape(g, 128, n, -1)
    if fmt == "e4m3":
        vals = words.view(ml_dtypes.float8_e4m3fn).astype(np.float64)
    else:
        nib = np.empty((g, 128, n, 4), np.uint8)
        nib[..., 0::2] = words & 0xF
        nib[..., 1::2] = words >> 4
        vals = E2M1[nib]
    vals = vals * np.repeat(np.exp2(scales.astype(np.float64) - 127.0), 8, axis=1)[..., None]
    return vals.transpose(0, 1, 3, 2).reshape(g * 512, n)


D, T, U, X, I, Q = 512, 1024, 1024, 1024, 512, 128


def setup_inputs():
    n = np.random.standard_normal
    idx = np.stack([np.random.permutation(T)[:I] for _ in range(8)])
    idx2 = np.stack([np.random.permutation(U)[:I] for _ in range(8)])
    idx3 = np.stack([np.random.permutation(X)[:I] for _ in range(8)])
    idx4 = np.stack([np.random.permutation(X)[:I] for _ in range(8)])
    idx5 = np.stack([np.random.permutation(X)[:I] for _ in range(8)])
    fd = mx_kscale(D)
    cachep = pack_weight(n((D, T)) / fd[:, None], "e4m3")
    draftp = pack_weight(n((D, U)) / fd[:, None], "e2m1")
    archp = pack_weight(n((D, X)) / fd[:, None], "e4m3")
    return {
        "query": (n((D, Q)) * 1.0 / np.sqrt(D) * fd[:, None]).astype(np.float32),
        "cache_words": cachep[0],
        "cache_scales": cachep[1],
        "draft_words": draftp[0],
        "draft_scales": draftp[1],
        "arch_words": archp[0],
        "arch_scales": archp[1],
        "offs": striped8(idx),
        "offs2": striped8(idx2),
        "offs3": striped8(idx3),
        "offs4": striped8(idx4),
        "offs5": striped8(idx5),
    }


def reference(query, cache_words, cache_scales, draft_words, draft_scales, arch_words, arch_scales, offs, offs2, offs3, offs4, offs5):
    idx = unstriped8(offs)
    idx2 = unstriped8(offs2)
    idx3 = unstriped8(offs3)
    idx4 = unstriped8(offs4)
    idx5 = unstriped8(offs5)
    cacheu = unpack_weight(cache_words, cache_scales, "e4m3")
    draftu = unpack_weight(draft_words, draft_scales, "e2m1")
    archu = unpack_weight(arch_words, arch_scales, "e4m3")
    queryq = mxq(f64(query), 0, "e4m3")
    a = queryq.T @ cacheu
    b = queryq.T @ draftu
    c0 = queryq.T @ archu
    w = np.minimum(pick8(a, idx, 16), pick8(b, idx2, 16))
    f1 = np.zeros((Q, X))
    f1[np.arange(Q)[:, None], idx3[np.arange(Q) % 128 // 16]] = w
    f2 = np.zeros((Q, X))
    f2[np.arange(Q)[:, None], idx4[np.arange(Q) % 128 // 16]] = pick8(b, idx2, 16)
    r = f1 - f2
    cc = np.maximum(c0, r)
    y = pick8(cc, idx5, 16) - w
    return y

@@ -1,0 +1,143 @@
+import concourse.mybir as mybir
+
+F32 = mybir.dt.float32
+BF16 = mybir.dt.bfloat16
+I32 = mybir.dt.int32
+U32 = mybir.dt.uint32
+U16 = mybir.dt.uint16
+U8 = mybir.dt.uint8
+FP8X4 = mybir.dt.float8_e4m3fn_x4
+FP4X4 = mybir.dt.float4_e2m1fn_x4
+ALU = mybir.AluOpType
+COPY = mybir.ActivationFunctionType.Copy
+
+P = 128
+PACK = 4
+D = 512
+Q = 128
+TOKENS = 1024
+SLOTS = 512
+HALF = SLOTS // 2
+LIST_COLS = SLOTS // 16
+BANK = 512
+DRAFT_N = 256
+
+FLOPS = 3 * 2 * D * Q * TOKENS
+
+
+def tile_attend_handover_three_kernel(tc, query, cache_words, cache_scales, draft_words, draft_scales,
+                                       arch_words, arch_scales, offs, offs2, offs3, offs4, offs5, out):
+    nc = tc.nc
+    with (
+        tc.tile_pool(name="lists", bufs=1) as lists,
+        tc.tile_pool(name="keep", bufs=1) as keep,
+        tc.psum_pool(name="psum", bufs=1) as psum,
+    ):
+        def load_list(name, source):
+            tile = lists.tile([P, LIST_COLS], U16, name=name)
+            nc.sync.dma_start(tile[:], source)
+            return tile
+
+        def zeroed_plane(name):
+            plane = keep.tile([P, TOKENS], U8, name=name, align_bytes=64)
+            nc.vector.memset(plane[:].bitcast(I32), 0)
+            return plane
+
+        def load_plane(plane, scales):
+            for quad in range(4):
+                nc.sync.dma_start(plane[32 * quad : 32 * quad + 4, :].bitcast(I32),
+                                  scales[0, 4 * quad : 4 * quad + 4, :].bitcast(I32))
+
+        def load_fp8_words(name, words):
+            tile = keep.tile([P, TOKENS], U32, name=name, align_bytes=64)
+            nc.sync.dma_start(tile[:].bitcast(I32), words[0].rearrange("p n t -> p (n t)").bitcast(I32))
+            return tile
+
+        def half_list(tile, h):
+            return tile[:, h * LIST_COLS // 2 : (h + 1) * LIST_COLS // 2]
+
+        def half(tile, h):
+            return tile[:, h * HALF : (h + 1) * HALF]
+
+        draft_plane = zeroed_plane("draft_plane")
+        cache_plane = zeroed_plane("cache_plane")
+        arch_plane = zeroed_plane("arch_plane")
+        f2 = keep.tile([P, TOKENS], F32, name="f2")
+        nc.vector.memset(f2[:], 0.0)
+        f1 = keep.tile([P, TOKENS], F32, name="f1")
+        nc.vector.memset(f1[:], 0.0)
+
+        q_raw = keep.tile([P, PACK, Q], F32, name="q_raw")
+        nc.sync.dma_start(q_raw[:], query.rearrange("(p j) q -> p j q", j=PACK))
+        draft = keep.tile([P, 2 * TOKENS], U8, name="draft", align_bytes=64)
+        nc.sync.dma_start(draft[:].bitcast(I32), draft_words[0].bitcast(I32))
+        idx2 = load_list("idx2", offs2)
+        load_plane(draft_plane, draft_scales)
+        cache = load_fp8_words("cache", cache_words)
+        idx4 = load_list("idx4", offs4)
+        load_plane(cache_plane, cache_scales)
+        idx = load_list("idx", offs)
+        idx3 = load_list("idx3", offs3)
+        arch = load_fp8_words("arch", arch_words)
+        load_plane(arch_plane, arch_scales)
+        idx5 = load_list("idx5", offs5)
+
+        q_bf = keep.tile([P, Q, PACK], BF16, name="q_bf", align_bytes=64)
+        nc.vector.tensor_copy(q_bf[:].rearrange("p (c i) j -> p c j i", i=4),
+                              q_raw[:].rearrange("p j (c i) -> p c j i", i=4))
+        q_codes = keep.tile([P, Q], U32, name="q_codes", align_bytes=64)
+        q_plane = keep.tile([P, Q], U8, name="q_plane", align_bytes=64)
+        nc.vector.quantize_mx(out=q_codes[:].bitcast(FP8X4), scales=q_plane[:],
+                              in_=q_bf[:].rearrange("p q j -> p (q j)"))
+
+        def scores(name, moving, plane):
+            bank = psum.tile([P, plane.shape[1]], F32, name=name)
+            nc.tensor.matmul_mx(out=bank[:], lhsT=q_codes[:].bitcast(FP8X4), lhsT_scale=q_plane[:],
+                                rhs=moving, rhs_scale=plane, start=True, stop=True)
+            return bank
+
+        b = keep.tile([P, TOKENS], F32, name="b", tag="scores")
+        for n in range(TOKENS // DRAFT_N):
+            cols = slice(n * DRAFT_N, (n + 1) * DRAFT_N)
+            bank = scores("b_bank%d" % n, draft[:, 2 * cols.start : 2 * cols.stop].bitcast(FP4X4), draft_plane[:, cols])
+            if n % 2 == 0:
+                nc.scalar.copy(b[:, cols], bank[:])
+            else:
+                nc.vector.tensor_copy(b[:, cols], bank[:])
+
+        b_picked = keep.tile([P, SLOTS], F32, name="b_picked")
+        for h in range(2):
+            nc.vector.tensor_copy(half(b_picked, h), b[:].indirect(half_list(idx2, h)))
+            nc.scalar.activation(f2[:].indirect(half_list(idx4, h)), half(b_picked, h), COPY)
+
+        a = keep.tile([P, TOKENS], F32, name="a", tag="scores")
+        for n in range(TOKENS // BANK):
+            cols = slice(n * BANK, (n + 1) * BANK)
+            bank = scores("a_bank%d" % n, cache[:, cols].bitcast(FP8X4), cache_plane[:, cols])
+            nc.vector.tensor_copy(a[:, cols], bank[:])
+
+        a_picked = keep.tile([P, SLOTS], F32, name="a_picked")
+        w = keep.tile([P, SLOTS], F32, name="w")
+        for h in range(2):
+            nc.vector.tensor_copy(half(a_picked, h), a[:].indirect(half_list(idx, h)))
+            nc.vector.tensor_tensor(half(w, h), half(a_picked, h), half(b_picked, h), ALU.min)
+            nc.scalar.activation(f1[:].indirect(half_list(idx3, h)), half(w, h), COPY)
+
+        r = keep.tile([P, TOKENS], F32, name="r")
+        cc = keep.tile([P, TOKENS], F32, name="cc")
+        c0_banks = []
+        for n in range(TOKENS // BANK):
+            cols = slice(n * BANK, (n + 1) * BANK)
+            c0_banks.append(scores("c0_bank%d" % n, arch[:, cols].bitcast(FP8X4), arch_plane[:, cols]))
+            nc.vector.tensor_tensor(r[:, cols], f1[:, cols], f2[:, cols], ALU.subtract)
+        for n in range(TOKENS // BANK):
+            cols = slice(n * BANK, (n + 1) * BANK)
+            nc.vector.tensor_tensor(cc[:, cols], r[:, cols], c0_banks[n][:], ALU.max)
+
+        y = keep.tile([P, SLOTS], F32, name="y")
+        cc_picked = keep.tile([P, HALF], F32, name="cc_picked")
+        nc.scalar.activation(cc_picked[:], cc[:].indirect(half_list(idx5, 1)), COPY)
+        nc.vector.tensor_tensor(half(y, 0), cc[:].indirect(half_list(idx5, 0)), half(w, 0), ALU.subtract)
+        nc.sync.dma_start(half(out, 0), half(y, 0))
+        nc.vector.tensor_tensor(half(y, 1), cc_picked[:], half(w, 1), ALU.subtract)
+        nc.sync.dma_start(half(out, 1), half(y, 1))

@@ -53,6 +53,11 @@ def tile_attend_handover_three_kernel(tc, query, cache_words, cache_scales, draf
             nc.sync.dma_start(tile[:].bitcast(I32), words[0].rearrange("p n t -> p (n t)").bitcast(I32))
             return tile
 
+        def zeroed_window(name, tag):
+            window = keep.tile([P, TOKENS], F32, name=name, tag=tag, align_bytes=64)
+            nc.vector.memset(window[:].bitcast(I32), 0)
+            return window
+
         def half_list(tile, h):
             return tile[:, h * LIST_COLS // 2 : (h + 1) * LIST_COLS // 2]
 
@@ -61,34 +66,30 @@ def tile_attend_handover_three_kernel(tc, query, cache_words, cache_scales, draf
 
         draft_plane = zeroed_plane("draft_plane")
         cache_plane = zeroed_plane("cache_plane")
-        arch_plane = zeroed_plane("arch_plane")
-        f2 = keep.tile([P, TOKENS], F32, name="f2")
-        nc.vector.memset(f2[:], 0.0)
-        f1 = keep.tile([P, TOKENS], F32, name="f1")
-        nc.vector.memset(f1[:], 0.0)
+        f2_parts = [zeroed_window("f2_0", "f2_0"), zeroed_window("f2_1", "f2_1")]
 
         q_raw = keep.tile([P, PACK, Q], F32, name="q_raw")
         nc.sync.dma_start(q_raw[:], query.rearrange("(p j) q -> p j q", j=PACK))
+        load_plane(draft_plane, draft_scales)
         draft = keep.tile([P, 2 * TOKENS], U8, name="draft", align_bytes=64)
         nc.sync.dma_start(draft[:].bitcast(I32), draft_words[0].bitcast(I32))
-        idx2 = load_list("idx2", offs2)
-        load_plane(draft_plane, draft_scales)
         cache = load_fp8_words("cache", cache_words)
-        idx4 = load_list("idx4", offs4)
+        idx2 = load_list("idx2", offs2)
         load_plane(cache_plane, cache_scales)
+        idx4 = load_list("idx4", offs4)
         idx = load_list("idx", offs)
         idx3 = load_list("idx3", offs3)
         arch = load_fp8_words("arch", arch_words)
-        load_plane(arch_plane, arch_scales)
         idx5 = load_list("idx5", offs5)
 
-        q_bf = keep.tile([P, Q, PACK], BF16, name="q_bf", align_bytes=64)
+        q_bf = keep.tile([P, Q, PACK], BF16, name="q_bf", tag="q_bf_f1", align_bytes=64)
         nc.vector.tensor_copy(q_bf[:].rearrange("p (c i) j -> p c j i", i=4),
                               q_raw[:].rearrange("p j (c i) -> p c j i", i=4))
         q_codes = keep.tile([P, Q], U32, name="q_codes", align_bytes=64)
         q_plane = keep.tile([P, Q], U8, name="q_plane", align_bytes=64)
         nc.vector.quantize_mx(out=q_codes[:].bitcast(FP8X4), scales=q_plane[:],
                               in_=q_bf[:].rearrange("p q j -> p (q j)"))
+        f1 = zeroed_window("f1", "q_bf_f1")
 
         def scores(name, moving, plane):
             bank = psum.tile([P, plane.shape[1]], F32, name=name)
@@ -96,32 +97,36 @@ def tile_attend_handover_three_kernel(tc, query, cache_words, cache_scales, draf
                                 rhs=moving, rhs_scale=plane, start=True, stop=True)
             return bank
 
-        b = keep.tile([P, TOKENS], F32, name="b", tag="scores")
+        b = keep.tile([P, TOKENS], F32, name="b")
         for n in range(TOKENS // DRAFT_N):
             cols = slice(n * DRAFT_N, (n + 1) * DRAFT_N)
             bank = scores("b_bank%d" % n, draft[:, 2 * cols.start : 2 * cols.stop].bitcast(FP4X4), draft_plane[:, cols])
-            if n % 2 == 0:
-                nc.scalar.copy(b[:, cols], bank[:])
-            else:
-                nc.vector.tensor_copy(b[:, cols], bank[:])
+            nc.scalar.copy(b[:, cols], bank[:])
+
+        arch_plane = draft_plane
+        load_plane(arch_plane, arch_scales)
+
+        a = keep.tile([P, TOKENS], F32, name="a")
+        a_banks = [scores("a_bank%d" % n, cache[:, n * BANK : (n + 1) * BANK].bitcast(FP8X4),
+                          cache_plane[:, n * BANK : (n + 1) * BANK]) for n in range(2)]
+        nc.scalar.copy(a[:, :BANK], a_banks[0][:])
 
         b_picked = keep.tile([P, SLOTS], F32, name="b_picked")
         for h in range(2):
             nc.vector.tensor_copy(half(b_picked, h), b[:].indirect(half_list(idx2, h)))
-            nc.scalar.activation(f2[:].indirect(half_list(idx4, h)), half(b_picked, h), COPY)
+            nc.scalar.activation(f2_parts[h][:].indirect(half_list(idx4, h)), half(b_picked, h), COPY)
+        nc.vector.tensor_copy(a[:, BANK:], a_banks[1][:])
 
-        a = keep.tile([P, TOKENS], F32, name="a", tag="scores")
-        for n in range(TOKENS // BANK):
-            cols = slice(n * BANK, (n + 1) * BANK)
-            bank = scores("a_bank%d" % n, cache[:, cols].bitcast(FP8X4), cache_plane[:, cols])
-            nc.vector.tensor_copy(a[:, cols], bank[:])
-
-        a_picked = keep.tile([P, SLOTS], F32, name="a_picked")
+        a_picked = keep.tile([P, SLOTS], F32, name="a_picked", tag="a_picked_f2")
         w = keep.tile([P, SLOTS], F32, name="w")
         for h in range(2):
             nc.vector.tensor_copy(half(a_picked, h), a[:].indirect(half_list(idx, h)))
+        for h in range(2):
             nc.vector.tensor_tensor(half(w, h), half(a_picked, h), half(b_picked, h), ALU.min)
-            nc.scalar.activation(f1[:].indirect(half_list(idx3, h)), half(w, h), COPY)
+        nc.scalar.activation(f1[:].indirect(idx3[:]), w[:], COPY)
+
+        f2 = keep.tile([P, TOKENS], F32, name="f2", tag="a_picked_f2")
+        nc.vector.tensor_tensor(f2[:], f2_parts[0][:], f2_parts[1][:], ALU.add)
 
         r = keep.tile([P, TOKENS], F32, name="r")
         cc = keep.tile([P, TOKENS], F32, name="cc")

@@ -48,9 +48,9 @@ def tile_attend_handover_three_kernel(tc, query, cache_words, cache_scales, draf
                 nc.sync.dma_start(plane[32 * quad : 32 * quad + 4, :].bitcast(I32),
                                   scales[0, 4 * quad : 4 * quad + 4, :].bitcast(I32))
 
-        def load_fp8_words(name, words):
-            tile = keep.tile([P, TOKENS], U32, name=name, align_bytes=64)
-            nc.sync.dma_start(tile[:].bitcast(I32), words[0].rearrange("p n t -> p (n t)").bitcast(I32))
+        def load_fp8_words(name, words, cols):
+            tile = keep.tile([P, cols.stop - cols.start], U32, name=name, align_bytes=64)
+            nc.sync.dma_start(tile[:].bitcast(I32), words[0].rearrange("p n t -> p (n t)").bitcast(I32)[:, cols])
             return tile
 
         def zeroed_window(name, tag):
@@ -70,44 +70,49 @@ def tile_attend_handover_three_kernel(tc, query, cache_words, cache_scales, draf
 
         q_raw = keep.tile([P, PACK, Q], F32, name="q_raw")
         nc.sync.dma_start(q_raw[:], query.rearrange("(p j) q -> p j q", j=PACK))
+        idx2 = load_list("idx2", offs2)
         load_plane(draft_plane, draft_scales)
         draft = keep.tile([P, 2 * TOKENS], U8, name="draft", align_bytes=64)
         nc.sync.dma_start(draft[:].bitcast(I32), draft_words[0].bitcast(I32))
-        cache = load_fp8_words("cache", cache_words)
-        idx2 = load_list("idx2", offs2)
+        cache = [load_fp8_words("cache_0", cache_words, slice(0, BANK))]
         load_plane(cache_plane, cache_scales)
+        cache.append(load_fp8_words("cache_1", cache_words, slice(BANK, TOKENS)))
         idx4 = load_list("idx4", offs4)
         idx = load_list("idx", offs)
         idx3 = load_list("idx3", offs3)
-        arch = load_fp8_words("arch", arch_words)
+        arch = load_fp8_words("arch", arch_words, slice(0, TOKENS))
         idx5 = load_list("idx5", offs5)
 
         q_bf = keep.tile([P, Q, PACK], BF16, name="q_bf", tag="q_bf_f1", align_bytes=64)
-        nc.vector.tensor_copy(q_bf[:].rearrange("p (c i) j -> p c j i", i=4),
-                              q_raw[:].rearrange("p j (c i) -> p c j i", i=4))
+        for copy, rows in ((nc.vector.tensor_copy, slice(0, Q // 2)), (nc.scalar.copy, slice(Q // 2, Q))):
+            copy(q_bf[:, rows, :].rearrange("p (c i) j -> p c j i", i=4),
+                 q_raw[:, :, rows].rearrange("p j (c i) -> p c j i", i=4))
         q_codes = keep.tile([P, Q], U32, name="q_codes", align_bytes=64)
         q_plane = keep.tile([P, Q], U8, name="q_plane", align_bytes=64)
         nc.vector.quantize_mx(out=q_codes[:].bitcast(FP8X4), scales=q_plane[:],
                               in_=q_bf[:].rearrange("p q j -> p (q j)"))
         f1 = zeroed_window("f1", "q_bf_f1")
 
-        def scores(name, moving, plane):
-            bank = psum.tile([P, plane.shape[1]], F32, name=name)
+        def scores(tag, moving, plane):
+            bank = psum.tile([P, plane.shape[1]], F32, name="bank", tag=tag)
             nc.tensor.matmul_mx(out=bank[:], lhsT=q_codes[:].bitcast(FP8X4), lhsT_scale=q_plane[:],
                                 rhs=moving, rhs_scale=plane, start=True, stop=True)
             return bank
 
         b = keep.tile([P, TOKENS], F32, name="b")
-        for n in range(TOKENS // DRAFT_N):
-            cols = slice(n * DRAFT_N, (n + 1) * DRAFT_N)
+        start = 0
+        for n, width in enumerate((256, 256, 256, 128, 128)):
+            cols = slice(start, start + width)
+            start = cols.stop
             bank = scores("b_bank%d" % n, draft[:, 2 * cols.start : 2 * cols.stop].bitcast(FP4X4), draft_plane[:, cols])
-            nc.scalar.copy(b[:, cols], bank[:])
+            copy = nc.vector.tensor_copy if n == 2 else nc.scalar.copy
+            copy(b[:, cols], bank[:])
 
         arch_plane = draft_plane
         load_plane(arch_plane, arch_scales)
 
         a = keep.tile([P, TOKENS], F32, name="a")
-        a_banks = [scores("a_bank%d" % n, cache[:, n * BANK : (n + 1) * BANK].bitcast(FP8X4),
+        a_banks = [scores("a_bank%d" % n, cache[n][:].bitcast(FP8X4),
                           cache_plane[:, n * BANK : (n + 1) * BANK]) for n in range(2)]
         nc.scalar.copy(a[:, :BANK], a_banks[0][:])
 
@@ -133,7 +138,7 @@ def tile_attend_handover_three_kernel(tc, query, cache_words, cache_scales, draf
         c0_banks = []
         for n in range(TOKENS // BANK):
             cols = slice(n * BANK, (n + 1) * BANK)
-            c0_banks.append(scores("c0_bank%d" % n, arch[:, cols].bitcast(FP8X4), arch_plane[:, cols]))
+            c0_banks.append(scores("b_bank%d" % n, arch[:, cols].bitcast(FP8X4), arch_plane[:, cols]))
             nc.vector.tensor_tensor(r[:, cols], f1[:, cols], f2[:, cols], ALU.subtract)
         for n in range(TOKENS // BANK):
             cols = slice(n * BANK, (n + 1) * BANK)

import concourse.mybir as mybir

F32 = mybir.dt.float32
BF16 = mybir.dt.bfloat16
I32 = mybir.dt.int32
U32 = mybir.dt.uint32
U16 = mybir.dt.uint16
U8 = mybir.dt.uint8
FP8X4 = mybir.dt.float8_e4m3fn_x4
FP4X4 = mybir.dt.float4_e2m1fn_x4
ALU = mybir.AluOpType
COPY = mybir.ActivationFunctionType.Copy

P = 128
PACK = 4
D = 512
Q = 128
TOKENS = 1024
SLOTS = 512
HALF = SLOTS // 2
LIST_COLS = SLOTS // 16
BANK = 512
DRAFT_N = 256

FLOPS = 3 * 2 * D * Q * TOKENS


def tile_attend_handover_three_kernel(tc, query, cache_words, cache_scales, draft_words, draft_scales,
                                       arch_words, arch_scales, offs, offs2, offs3, offs4, offs5, out):
    nc = tc.nc
    with (
        tc.tile_pool(name="lists", bufs=1) as lists,
        tc.tile_pool(name="keep", bufs=1) as keep,
        tc.psum_pool(name="psum", bufs=1) as psum,
    ):
        def load_list(name, source):
            tile = lists.tile([P, LIST_COLS], U16, name=name)
            nc.sync.dma_start(tile[:], source)
            return tile

        def zeroed_plane(name):
            plane = keep.tile([P, TOKENS], U8, name=name, align_bytes=64)
            nc.vector.memset(plane[:].bitcast(I32), 0)
            return plane

        def load_plane(plane, scales):
            for quad in range(4):
                nc.sync.dma_start(plane[32 * quad : 32 * quad + 4, :].bitcast(I32),
                                  scales[0, 4 * quad : 4 * quad + 4, :].bitcast(I32))

        def load_fp8_words(name, words, cols):
            tile = keep.tile([P, cols.stop - cols.start], U32, name=name, align_bytes=64)
            nc.sync.dma_start(tile[:].bitcast(I32), words[0].rearrange("p n t -> p (n t)").bitcast(I32)[:, cols])
            return tile

        def zeroed_window(name, tag):
            window = keep.tile([P, TOKENS], F32, name=name, tag=tag, align_bytes=64)
            nc.vector.memset(window[:].bitcast(I32), 0)
            return window

        def half_list(tile, h):
            return tile[:, h * LIST_COLS // 2 : (h + 1) * LIST_COLS // 2]

        def half(tile, h):
            return tile[:, h * HALF : (h + 1) * HALF]

        draft_plane = zeroed_plane("draft_plane")
        cache_plane = zeroed_plane("cache_plane")
        f2_parts = [zeroed_window("f2_0", "f2_0"), zeroed_window("f2_1", "f2_1")]

        q_raw = keep.tile([P, PACK, Q], F32, name="q_raw")
        nc.sync.dma_start(q_raw[:], query.rearrange("(p j) q -> p j q", j=PACK))
        idx2 = load_list("idx2", offs2)
        load_plane(draft_plane, draft_scales)
        draft = keep.tile([P, 2 * TOKENS], U8, name="draft", align_bytes=64)
        nc.sync.dma_start(draft[:].bitcast(I32), draft_words[0].bitcast(I32))
        cache = [load_fp8_words("cache_0", cache_words, slice(0, BANK))]
        load_plane(cache_plane, cache_scales)
        cache.append(load_fp8_words("cache_1", cache_words, slice(BANK, TOKENS)))
        idx4 = load_list("idx4", offs4)
        idx = load_list("idx", offs)
        idx3 = load_list("idx3", offs3)
        arch = load_fp8_words("arch", arch_words, slice(0, TOKENS))
        idx5 = load_list("idx5", offs5)

        q_bf = keep.tile([P, Q, PACK], BF16, name="q_bf", tag="q_bf_f1", align_bytes=64)
        for copy, rows in ((nc.vector.tensor_copy, slice(0, Q // 2)), (nc.scalar.copy, slice(Q // 2, Q))):
            copy(q_bf[:, rows, :].rearrange("p (c i) j -> p c j i", i=4),
                 q_raw[:, :, rows].rearrange("p j (c i) -> p c j i", i=4))
        q_codes = keep.tile([P, Q], U32, name="q_codes", align_bytes=64)
        q_plane = keep.tile([P, Q], U8, name="q_plane", align_bytes=64)
        nc.vector.quantize_mx(out=q_codes[:].bitcast(FP8X4), scales=q_plane[:],
                              in_=q_bf[:].rearrange("p q j -> p (q j)"))
        f1 = zeroed_window("f1", "q_bf_f1")

        def scores(tag, moving, plane):
            bank = psum.tile([P, plane.shape[1]], F32, name="bank", tag=tag)
            nc.tensor.matmul_mx(out=bank[:], lhsT=q_codes[:].bitcast(FP8X4), lhsT_scale=q_plane[:],
                                rhs=moving, rhs_scale=plane, start=True, stop=True)
            return bank

        b = keep.tile([P, TOKENS], F32, name="b")
        start = 0
        for n, width in enumerate((256, 256, 256, 128, 128)):
            cols = slice(start, start + width)
            start = cols.stop
            bank = scores("b_bank%d" % n, draft[:, 2 * cols.start : 2 * cols.stop].bitcast(FP4X4), draft_plane[:, cols])
            copy = nc.vector.tensor_copy if n == 2 else nc.scalar.copy
            copy(b[:, cols], bank[:])

        arch_plane = draft_plane
        load_plane(arch_plane, arch_scales)

        a = keep.tile([P, TOKENS], F32, name="a")
        a_banks = [scores("a_bank%d" % n, cache[n][:].bitcast(FP8X4),
                          cache_plane[:, n * BANK : (n + 1) * BANK]) for n in range(2)]
        nc.scalar.copy(a[:, :BANK], a_banks[0][:])

        b_picked = keep.tile([P, SLOTS], F32, name="b_picked")
        for h in range(2):
            nc.vector.tensor_copy(half(b_picked, h), b[:].indirect(half_list(idx2, h)))
            nc.scalar.activation(f2_parts[h][:].indirect(half_list(idx4, h)), half(b_picked, h), COPY)
        nc.vector.tensor_copy(a[:, BANK:], a_banks[1][:])

        a_picked = keep.tile([P, SLOTS], F32, name="a_picked", tag="a_picked_f2")
        w = keep.tile([P, SLOTS], F32, name="w")
        for h in range(2):
            nc.vector.tensor_copy(half(a_picked, h), a[:].indirect(half_list(idx, h)))
        for h in range(2):
            nc.vector.tensor_tensor(half(w, h), half(a_picked, h), half(b_picked, h), ALU.min)
        nc.scalar.activation(f1[:].indirect(idx3[:]), w[:], COPY)

        f2 = keep.tile([P, TOKENS], F32, name="f2", tag="a_picked_f2")
        nc.vector.tensor_tensor(f2[:], f2_parts[0][:], f2_parts[1][:], ALU.add)

        r = keep.tile([P, TOKENS], F32, name="r")
        cc = keep.tile([P, TOKENS], F32, name="cc")
        c0_banks = []
        for n in range(TOKENS // BANK):
            cols = slice(n * BANK, (n + 1) * BANK)
            c0_banks.append(scores("b_bank%d" % n, arch[:, cols].bitcast(FP8X4), arch_plane[:, cols]))
            nc.vector.tensor_tensor(r[:, cols], f1[:, cols], f2[:, cols], ALU.subtract)
        for n in range(TOKENS // BANK):
            cols = slice(n * BANK, (n + 1) * BANK)
            nc.vector.tensor_tensor(cc[:, cols], r[:, cols], c0_banks[n][:], ALU.max)

        y = keep.tile([P, SLOTS], F32, name="y")
        cc_picked = keep.tile([P, HALF], F32, name="cc_picked")
        nc.scalar.activation(cc_picked[:], cc[:].indirect(half_list(idx5, 1)), COPY)
        nc.vector.tensor_tensor(half(y, 0), cc[:].indirect(half_list(idx5, 0)), half(w, 0), ALU.subtract)
        nc.sync.dma_start(half(out, 0), half(y, 0))
        nc.vector.tensor_tensor(half(y, 1), cc_picked[:], half(w, 1), ALU.subtract)
        nc.sync.dma_start(half(out, 1), half(y, 1))
